import numpy as np
import ml_dtypes


def mxq(x, axis, fmt="e4m3"):
    dtype, down = {"e4m3": (ml_dtypes.float8_e4m3fn, 7), "e5m2": (ml_dtypes.float8_e5m2, 14)}[fmt]
    v = np.moveaxis(np.asarray(x, np.float32).astype(ml_dtypes.bfloat16).astype(np.float64), axis, -1)
    blocks = v.reshape(v.shape[:-1] + (-1, 32))
    amax = np.abs(blocks).max(-1, keepdims=True)
    byte = np.maximum(np.where(amax > 0, np.frexp(amax)[1] - 1 + 127, 0) - down, 1)
    scale = np.exp2(byte - 127.0)
    codes = (blocks / scale).astype(np.float32).astype(dtype).astype(np.float64)
    return np.moveaxis((codes * scale).reshape(v.shape), -1, axis)


WIDE = False


def mx_kscale(k):
    if not WIDE:
        return np.ones(k)
    levels = np.array([10, -10, 5, -5, 0])
    if k % 512:
        return np.exp2(np.random.permutation(np.resize(levels, k // 32))).repeat(32)
    a = np.empty((k // 512, 16))
    for p in range(k // 512):
        a[p, :8] = np.random.permutation(np.resize(levels, 8))
        for g in range(8):
            far = levels[np.abs(levels - a[p, g]) >= 10]
            a[p, g + 8] = far[np.random.randint(len(far))]
    return np.exp2(a.ravel()).repeat(32)


BF16 = ml_dtypes.bfloat16


def bf(x):
    return np.asarray(x, np.float32).astype(BF16)


def f64(x):
    return np.asarray(x).astype(np.float64)


E2M1 = np.array([0.0, 0.5, 1.0, 1.5, 2.0, 3.0, 4.0, 6.0, -0.0, -0.5, -1.0, -1.5, -2.0, -3.0, -4.0, -6.0])


def pack_weight(w, fmt):
    k, n = w.shape
    w = f64(bf(w)).reshape(k // 32, 32, n)
    amax = np.abs(w).max(1)
    if fmt == "e4m3":
        byte = np.frexp(amax)[1] - 1 + 127 - 7
    else:
        mant, ex = np.frexp(amax / 6.0)
        byte = np.where(mant > 0.5, ex, ex - 1) + 127
    byte = np.clip(np.where(amax > 0, byte, 1), 1, 254)
    scaled = (w * np.exp2(127.0 - byte)[:, None, :]).reshape(k, n).astype(np.float32)
    by_word = np.ascontiguousarray(scaled.reshape(k // 512, 128, 4, n).transpose(0, 1, 3, 2))
    if fmt == "e4m3":
        words = by_word.astype(ml_dtypes.float8_e4m3fn).view(np.uint8)
    else:
        c = by_word.astype(ml_dtypes.float4_e2m1fn).view(np.uint8) & 0xF
        words = c[..., 0::2] | (c[..., 1::2] << 4)
    return np.ascontiguousarray(words), np.ascontiguousarray(byte.astype(np.uint8).reshape(k // 512, 16, n))


def unpack_weight(words, scales, fmt):
    g, p, n, _ = words.shape
    if fmt == "e4m3":
        vals = np.ascontiguousarray(words).view(ml_dtypes.float8_e4m3fn).astype(np.float64)
    else:
        nib = np.empty((g, p, n, 4), np.uint8)
        nib[..., 0::2] = words & 0xF
        nib[..., 1::2] = words >> 4
        vals = E2M1[nib]
    vals = vals * np.repeat(np.exp2(scales.astype(np.float64) - 127.0), 8, axis=1)[..., None]
    return vals.transpose(0, 1, 3, 2).reshape(g * 512, n)
def pack4(w):
    words, scales = pack_weight(w, "e2m1")
    return words.reshape(words.shape[0], 128, -1), scales


def unpack4(words, scales):
    return unpack_weight(words.reshape(words.shape[0], 128, -1, 2), scales, "e2m1")


V, S, P = 1024, 1536, 512


def setup_inputs():
    s, u = mx_kscale(S), mx_kscale(V)
    a = np.random.standard_normal((S, S)) * 0.35 / np.sqrt(S) / s[:, None] * s
    f = np.random.standard_normal((V, V)) * 0.35 / np.sqrt(V) / u[:, None]
    b = np.random.standard_normal((S, P)) / np.sqrt(S) / s[:, None]
    a_words, a_scales = pack4(a)
    f_words, f_scales = pack4(f)
    b_words, b_scales = pack4(b)
    return {"c": bf(np.random.standard_normal((V, S)) * s),
            "a_words": a_words, "a_scales": a_scales,
            "vol": bf(np.random.uniform(0.5, 1.5, V) * u),
            "f_words": f_words, "f_scales": f_scales,
            "b_words": b_words, "b_scales": b_scales,
            "theta": bf(0.5 * np.random.standard_normal(V)),
            "y0": bf(0.5 * np.random.standard_normal((V, P)))}


def reference(c, a_words, a_scales, vol, f_words, f_scales, b_words, b_scales, theta, y0):
    c = f64(c)
    A = unpack4(a_words, a_scales)
    F = unpack4(f_words, f_scales)
    B = unpack4(b_words, b_scales)
    c1 = c + (mxq(c, 1, "e4m3") @ A)
    n = f64(vol)[:, None] * c1
    c2 = c1 + (F.T @ mxq(n, 0, "e4m3"))
    gate = np.exp(f64(theta))[:, None]
    return f64(y0) + gate * (mxq(c2, 1, "e4m3") @ B)

@@ -1,0 +1,412 @@
+from contextlib import ExitStack
+
+import concourse.mybir as mybir
+from concourse.masks import make_identity
+
+V, S, J = 1024, 1536, 512
+FLOPS = 2 * V * S * S + 2 * V * V * S + 2 * V * S * J
+
+F32 = mybir.dt.float32
+BF16 = mybir.dt.bfloat16
+I32 = mybir.dt.int32
+U32 = mybir.dt.uint32
+U8 = mybir.dt.uint8
+FP8X4 = mybir.dt.float8_e4m3fn_x4
+FP4X4 = mybir.dt.float4_e2m1fn_x4
+ADD = mybir.AluOpType.add
+MULT = mybir.AluOpType.mult
+COPY = mybir.ActivationFunctionType.Copy
+EXP = mybir.ActivationFunctionType.Exp
+
+P = 128
+EVAC_C = ('scalar', 'vector', 'scalar')
+EVAC_2 = (('vector', 'scalar', 'vector', 'scalar'), ('scalar', 'scalar', 'scalar', 'scalar'), ('scalar', 'scalar', 'scalar', 'vector'))
+INTER = (('scalar', 'scalar', 'scalar', 'scalar'), ('scalar', 'scalar', 'scalar', 'vector'), ('scalar', 'scalar', 'scalar', 'scalar'))
+LAG_QC = 1
+LAG_M = 2
+LAG_I = (0, 0, 2, 2)
+LAG_QM = 5
+LAG_Q2 = 2
+NV = V // P
+NS = S // 512
+NG = V // 512
+
+
+def tile_reactor_network_steps_t2_kernel(
+    tc, c, a_words, a_scales, vol, f_words, f_scales, b_words, b_scales, theta, y0, out
+):
+    nc = tc.nc
+    with ExitStack() as ctx:
+        keep = ctx.enter_context(tc.tile_pool(name="keep", bufs=1))
+        work = ctx.enter_context(tc.tile_pool(name="work", bufs=2))
+        psum = ctx.enter_context(tc.psum_pool(name="psum", bufs=8))
+
+        c_sb = []
+        for i in range(NV):
+            c_tile = keep.tile([P, S], BF16, tag="c_in%d" % i, name="c_tile", align_bytes=64)
+            c_sb.append(c_tile)
+        a_sb = keep.tile([P, NS, 2 * S], U8, align_bytes=64)
+        a_sc = keep.tile([P, NS, S], U8, align_bytes=64)
+        f_raw = keep.tile([P, NG, 2 * V], U8, align_bytes=64)
+        f_sb = keep.tile([P, NG, 2 * V], U8, align_bytes=64)
+        fs_raw = keep.tile([P, NG, V], U8, align_bytes=64)
+        f_sc = keep.tile([P, NG, V], U8, align_bytes=64)
+        b_sb = keep.tile([P, NS, 2 * J], U8, align_bytes=64)
+        b_sc = keep.tile([P, NS, J], U8, align_bytes=64)
+        cq = keep.tile([P, NS, V], U32, align_bytes=64)
+        cq_sc = keep.tile([P, NS, V], U8, align_bytes=64)
+        mq = keep.tile([P, NS, NG, 512], U32, align_bytes=64)
+        mq_sc = keep.tile([P, NS, NG, 512], U8, align_bytes=64)
+        c2q = keep.tile([P, NS, V], U32, align_bytes=64)
+        c2q_sc = keep.tile([P, NS, V], U8, align_bytes=64)
+        c1 = keep.tile([P, NV, S], F32, align_bytes=64)
+        y_sb = keep.tile([P, NV, J], BF16, align_bytes=64)
+        ident = keep.tile([P, P], F32, align_bytes=64)
+        ident_b = keep.tile([P, P], BF16, align_bytes=64)
+        vt_rows = keep.tile([P, 512], BF16, align_bytes=64)
+        vt_cols = keep.tile([P, 2, NV], F32)
+        vol_f = vt_cols[:, 0, :]
+        gate = keep.tile([P, NV], F32)
+        warm = keep.tile([P, 1], F32)
+
+        with tc.manual_schedule():
+            c_rows = c.rearrange("(g p t) s -> p g t s", p=P, t=4)
+            y_rows = y0.rearrange("(g p t) j -> p g t j", p=P, t=4)
+            out_rows = out.rearrange("(g p t) j -> p g t j", p=P, t=4)
+
+            def load_c(i):
+                nc.sync.dma_start(out=c_sb[i][:], in_=c_rows[:, i // 4, i % 4, :])
+
+            def load_planes(plane, scales, lo, hi, queue=nc.sync):
+                for q in range(4):
+                    queue.dma_start(
+                        out=plane[32 * q : 32 * q + 4, :, lo:hi].bitcast(I32),
+                        in_=scales[:, 4 * q : 4 * q + 4, lo:hi].rearrange("a r n -> r a n").bitcast(I32),
+                    )
+
+            def load_a(n):
+                cols = slice(1024 * n, 1024 * (n + 1))
+                nc.sync.dma_start(
+                    out=a_sb[:, :, cols].bitcast(I32),
+                    in_=a_words[:, :, cols].rearrange("a p w -> p a w").bitcast(I32),
+                )
+
+            nc.vector.memset(vt_rows[:], 0.0)
+            make_identity(nc, ident[:])
+            nc.gpsimd.tensor_copy(out=ident_b[:], in_=ident[:])
+            nc.scalar.dma_start(out=vt_rows[0:NG, :], in_=vol.rearrange("(g r) -> g r", g=NG))
+            nc.scalar.dma_start(out=vt_rows[NG : 2 * NG, :], in_=theta.rearrange("(g r) -> g r", g=NG))
+            nc.vector.memset(a_sc[:].rearrange("p a n -> p (a n)").bitcast(I32), 0)
+            nc.gpsimd.memset(fs_raw[:].rearrange("p a n -> p (a n)").bitcast(I32), 0)
+            nc.gpsimd.memset(b_sc[:].rearrange("p a n -> p (a n)").bitcast(I32), 0)
+            load_planes(a_sc, a_scales, 0, 512, nc.scalar)
+            for i in range(4):
+                load_c(i)
+            load_a(0)
+            for i in range(4, NV):
+                load_c(i)
+            load_planes(fs_raw, f_scales, 0, V)
+            nc.sync.dma_start(out=f_raw[:].bitcast(I32), in_=f_words.rearrange("g p w -> p g w").bitcast(I32))
+            load_planes(a_sc, a_scales, 512, S)
+            load_a(1)
+            load_planes(b_sc, b_scales, 0, J)
+            load_a(2)
+            nc.sync.dma_start(out=b_sb[:].bitcast(I32), in_=b_words.rearrange("g p w -> p g w").bitcast(I32))
+            for g in range(NG):
+                nc.sync.dma_start(out=y_sb[:, 4 * g : 4 * g + 4, :], in_=y_rows[:, g, :, :])
+            nc.vector.memset(warm[:], 0.0)
+            nc.scalar.activation(out=warm[:], in_=warm[:], func=EXP)
+
+            todo = {}
+            clock = [0]
+
+            def later(lag, fn, *args):
+                todo.setdefault(clock[0] + lag, []).append((fn, args))
+
+            def tick():
+                for fn, args in todo.get(clock[0], []):
+                    fn(*args)
+                clock[0] += 1
+
+            def spread(bank, grouped, engine):
+                dst = grouped[:].bitcast(F32).rearrange("p (k r) u -> p k r u", k=2)
+                src = bank[:].rearrange("p k u r -> p k r u")
+                if engine == "scalar":
+                    nc.scalar.copy(out=dst, in_=src)
+                else:
+                    nc.vector.tensor_copy(out=dst, in_=src)
+
+            def quant(grouped, codes, scales):
+                nc.vector.quantize_mx(
+                    out=codes.bitcast(FP8X4), scales=scales, in_=grouped[:].rearrange("p r t -> p (r t)")
+                )
+
+            def transposes_c(j):
+                banks = []
+                c_words = [c_sb[2 * j + k][:].bitcast(F32) for k in range(2)]
+                for a in range(NS):
+                    bank = psum.tile([P, 2, 2, P], F32, tag="bank", name="bank")
+                    banks.append(bank)
+                for k in range(2):
+                    for a in range(NS):
+                        for u in range(2):
+                            lo = 256 * a + u
+                            nc.tensor.transpose(
+                                banks[a][:, k, u, :], c_words[k][:, lo : 256 * (a + 1) : 2], ident[:]
+                            )
+                later(0, evac_c, j, banks)
+
+            def evac_c(j, banks):
+                groups = []
+                for a in range(NS):
+                    grouped = work.tile([P, 2 * P, 4], BF16, tag="grouped", name="grouped", bufs=6, align_bytes=64)
+                    spread(banks[a], grouped, EVAC_C[a])
+                    groups.append(grouped)
+                later(LAG_QC, quant_c, j, groups)
+
+            def quant_c(j, groups):
+                cols = slice(2 * P * j, 2 * P * (j + 1))
+                for a in range(NS):
+                    quant(groups[a], cq[:, a, cols], cq_sc[:, a, cols])
+
+            def stage1(n, i):
+                acc = psum.tile([P, 512], F32, tag="bank", name="acc")
+                rows = slice(P * i, P * (i + 1))
+                for a in range(NS):
+                    nc.tensor.matmul_mx(
+                        out=acc[:],
+                        lhsT=cq[:, a, rows].bitcast(FP8X4),
+                        lhsT_scale=cq_sc[:, a, rows],
+                        rhs=a_sb[:, a, 1024 * n : 1024 * (n + 1)].bitcast(FP4X4),
+                        rhs_scale=a_sc[:, a, 512 * n : 512 * (n + 1)],
+                        start=(a == 0),
+                        stop=(a == NS - 1),
+                    )
+                later(0, add_c, n, i, acc)
+
+            mlins = {}
+
+            def add_c(n, i, acc):
+                cols = slice(512 * n, 512 * (n + 1))
+                nc.vector.tensor_tensor(
+                    out=c1[:, i, cols].rearrange("p (u w e) -> p u w e", u=2, e=2),
+                    in0=acc[:].rearrange("p (w u e) -> p u w e", u=2, e=2),
+                    in1=c_sb[i][:, cols].rearrange("p (w u e) -> p u w e", u=2, e=2),
+                    op=ADD,
+                )
+                later(LAG_M, amounts, n, i)
+
+            def amounts(n, i):
+                cols = slice(512 * n, 512 * (n + 1))
+                if i % 4 == 0:
+                    mlin = work.tile([P, 4, 512], BF16, tag="mlin", name="mlin", bufs=2, align_bytes=64)
+                    mlins[0] = mlin
+                mlin = mlins[0]
+                nc.scalar.activation(
+                    out=mlin[:, i % 4, :], in_=c1[:, i, cols], func=COPY, scale=vol_f[:, i : i + 1]
+                )
+                if i % 4 == 3:
+                    mint = work.tile([P, 512, 4], BF16, tag="mint", name="mint", bufs=2, align_bytes=64)
+                    for h in range(4):
+                        later(LAG_I[h], interleave, n, mlin, mint, h)
+                    later(LAG_QM, quant_m, n, i // 4, mint)
+
+            def interleave(n, mlin, mint, h):
+                cols = slice(128 * h, 128 * (h + 1))
+                dst = mint[:, cols, :]
+                src = mlin[:, :, cols].rearrange("p t s -> p s t")
+                if INTER[n][h] == "scalar":
+                    nc.scalar.copy(out=dst, in_=src)
+                else:
+                    nc.vector.tensor_copy(out=dst, in_=src)
+
+            def quant_m(n, g, mint):
+                quant(mint, mq[:, n, g, :], mq_sc[:, n, g, :])
+
+            pairs = {}
+
+            def stage2(n, i):
+                acc = psum.tile([P, 512], F32, tag="bank", name="acc")
+                for g in range(NG):
+                    nc.tensor.matmul_mx(
+                        out=acc[:],
+                        lhsT=f_sb[:, g, 256 * i : 256 * (i + 1)].bitcast(FP4X4),
+                        lhsT_scale=f_sc[:, g, P * i : P * (i + 1)],
+                        rhs=mq[:, n, g, :].bitcast(FP8X4),
+                        rhs_scale=mq_sc[:, n, g, :],
+                        start=(g == 0),
+                        stop=(g == NG - 1),
+                    )
+                later(0, add_c1, n, i, acc)
+
+            def add_c1(n, i, acc):
+                if i % 2 == 0:
+                    c2 = work.tile([P, 2, 512], BF16, tag="c2", name="c2", bufs=8, align_bytes=64)
+                    pairs[(n, i // 2)] = c2
+                c2 = pairs[(n, i // 2)]
+                nc.vector.tensor_tensor(
+                    out=c2[:, i % 2, :], in0=acc[:], in1=c1[:, i, 512 * n : 512 * (n + 1)], op=ADD
+                )
+
+            def transposes_2(n, j):
+                c2 = pairs[(n, j)]
+                words = c2[:].bitcast(F32)
+                bank = psum.tile([P, 2, 2, P], F32, tag="bank", name="bank")
+                for k in range(2):
+                    for u in range(2):
+                        nc.tensor.transpose(bank[:, k, u, :], words[:, k, P * u : P * (u + 1)], ident[:])
+                later(0, evac_2, n, j, bank)
+
+            def evac_2(n, j, bank):
+                grouped = work.tile([P, 2 * P, 4], BF16, tag="grouped", name="grouped", bufs=6, align_bytes=64)
+                spread(bank, grouped, EVAC_2[n][j])
+                later(LAG_Q2, quant_2, n, j, grouped)
+
+            def quant_2(n, j, grouped):
+                cols = slice(2 * P * j, 2 * P * (j + 1))
+                quant(grouped, c2q[:, n, cols], c2q_sc[:, n, cols])
+
+            accs = {}
+
+            def stage3(i, first, last):
+                if first == 0:
+                    acc = psum.tile([P, 512], F32, tag="bank", name="acc")
+                    accs[i] = acc
+                acc = accs[i]
+                rows = slice(P * i, P * (i + 1))
+                for n in range(first, last):
+                    nc.tensor.matmul_mx(
+                        out=acc[:],
+                        lhsT=c2q[:, n, rows].bitcast(FP8X4),
+                        lhsT_scale=c2q_sc[:, n, rows],
+                        rhs=b_sb[:, n, :].bitcast(FP4X4),
+                        rhs_scale=b_sc[:, n, :],
+                        start=(n == 0),
+                        stop=(n == NS - 1),
+                    )
+                if last == NS:
+                    later(0, finish, i, acc)
+
+            def finish(i, acc):
+                res = work.tile([P, 512], F32, tag="res", name="res", bufs=4, align_bytes=64)
+                nc.vector.scalar_tensor_tensor(
+                    out=res[:], in0=acc[:], scalar=gate[:, i : i + 1], in1=y_sb[:, i, :], op0=MULT, op1=ADD
+                )
+                nc.sync.dma_start(out=out_rows[:, i // 4, i % 4, :], in_=res[:])
+
+            def permute_f(g, h):
+                if h < 2:
+                    cols = slice(1024 * h, 1024 * (h + 1))
+                    nc.vector.tensor_copy(
+                        out=f_sb[:, g, cols].rearrange("p (t m b) -> p t m b", t=4, b=2),
+                        in_=f_raw[:, g, cols].rearrange("p (m t b) -> p t m b", t=4, b=2),
+                    )
+                else:
+                    for h2 in range(2):
+                        cols = slice(512 * h2, 512 * (h2 + 1))
+                        nc.vector.tensor_copy(
+                            out=f_sc[:, g, cols].rearrange("p (t m) -> p t m", t=4),
+                            in_=fs_raw[:, g, cols].rearrange("p (m t) -> p t m", t=4),
+                        )
+
+            def vectors():
+                bank = psum.tile([P, 4, P], BF16, tag="bank", name="bank")
+                for k in range(4):
+                    nc.tensor.transpose(bank[:, k, :], vt_rows[:, k:512:4], ident_b[:])
+                nc.vector.tensor_copy(
+                    out=vt_cols[:].rearrange("p v (g t) -> p v g t", g=NG),
+                    in_=bank[:, :, 0 : 2 * NG].rearrange("p t (v g) -> p v g t", g=NG),
+                )
+                nc.scalar.activation(out=gate[:], in_=vt_cols[:, 1, :], func=EXP)
+
+            def unit(fn, *args):
+                fn(*args)
+                tick()
+
+            unit(transposes_c, 0)
+            unit(transposes_c, 1)
+            vectors()
+            unit(stage1, 0, 0)
+            unit(stage1, 0, 1)
+            unit(transposes_c, 2)
+            unit(stage1, 0, 2)
+            unit(stage1, 0, 3)
+            unit(transposes_c, 3)
+            unit(stage1, 0, 4)
+            permute_f(0, 0)
+            unit(stage1, 0, 5)
+            permute_f(0, 1)
+            unit(stage1, 0, 6)
+            permute_f(0, 2)
+            unit(stage1, 0, 7)
+            permute_f(1, 0)
+            unit(stage1, 1, 0)
+            permute_f(1, 1)
+            unit(stage1, 1, 1)
+            permute_f(1, 2)
+            unit(stage1, 1, 2)
+            unit(stage1, 1, 3)
+            unit(stage1, 1, 4)
+            unit(stage1, 1, 5)
+            unit(stage1, 1, 6)
+            unit(stage1, 1, 7)
+            unit(stage2, 0, 0)
+            unit(stage1, 2, 0)
+            unit(stage2, 0, 1)
+            unit(stage1, 2, 1)
+            unit(stage2, 0, 2)
+            unit(stage1, 2, 2)
+            unit(stage2, 0, 3)
+            unit(stage1, 2, 3)
+            unit(stage2, 0, 4)
+            unit(stage1, 2, 4)
+            unit(stage2, 0, 5)
+            unit(stage1, 2, 5)
+            unit(stage2, 0, 6)
+            transposes_2(0, 0)
+            unit(transposes_2, 0, 1)
+            unit(stage1, 2, 6)
+            unit(stage2, 0, 7)
+            unit(stage1, 2, 7)
+            unit(stage2, 1, 0)
+            unit(stage2, 1, 1)
+            unit(stage2, 1, 2)
+            unit(stage2, 1, 3)
+            transposes_2(0, 2)
+            unit(transposes_2, 0, 3)
+            unit(stage2, 1, 4)
+            unit(stage2, 1, 5)
+            unit(stage2, 1, 6)
+            transposes_2(1, 0)
+            unit(transposes_2, 1, 1)
+            unit(stage2, 1, 7)
+            unit(transposes_2, 1, 2)
+            unit(transposes_2, 1, 3)
+            for k in range(2):
+                            tick()
+            unit(stage3, 0, 0, 2)
+            unit(stage3, 1, 0, 2)
+            unit(stage3, 2, 0, 2)
+            unit(stage3, 3, 0, 2)
+            unit(stage2, 2, 0)
+            unit(stage2, 2, 1)
+            unit(stage2, 2, 2)
+            unit(stage2, 2, 3)
+            unit(stage2, 2, 4)
+            unit(transposes_2, 2, 0)
+            unit(stage2, 2, 5)
+            unit(stage2, 2, 6)
+            unit(transposes_2, 2, 1)
+            unit(stage2, 2, 7)
+            unit(stage3, 0, 2, 3)
+            unit(stage3, 1, 2, 3)
+            unit(transposes_2, 2, 2)
+            unit(stage3, 2, 2, 3)
+            unit(stage3, 3, 2, 3)
+            unit(transposes_2, 2, 3)
+            unit(stage3, 4, 0, 3)
+            unit(stage3, 5, 0, 3)
+            unit(stage3, 6, 0, 3)
+            unit(stage3, 7, 0, 3)
+            for k in range(8):
+                            tick()

@@ -19,14 +19,15 @@ COPY = mybir.ActivationFunctionType.Copy
 EXP = mybir.ActivationFunctionType.Exp
 
 P = 128
-EVAC_C = ('scalar', 'vector', 'scalar')
-EVAC_2 = (('vector', 'scalar', 'vector', 'scalar'), ('scalar', 'scalar', 'scalar', 'scalar'), ('scalar', 'scalar', 'scalar', 'vector'))
+EVAC_C = ('vector', 'scalar', 'scalar')
+SHUF = (0, 0, 0, 0, 'scalar', 0, 0, 'vector')
+EVAC_2 = (('vector', 'scalar', 'scalar', 'scalar'), ('scalar', 'scalar', 'scalar', 'scalar'), ('vector', 'scalar', 'scalar', 'vector'))
 INTER = (('scalar', 'scalar', 'scalar', 'scalar'), ('scalar', 'scalar', 'scalar', 'vector'), ('scalar', 'scalar', 'scalar', 'scalar'))
 LAG_QC = 1
-LAG_M = 2
-LAG_I = (0, 0, 2, 2)
-LAG_QM = 5
-LAG_Q2 = 2
+LAG_M = 1
+LAG_I = (1, 1, 2, 2)
+LAG_QM = 6
+LAG_Q2 = 3
 NV = V // P
 NS = S // 512
 NG = V // 512
@@ -45,8 +46,12 @@ def tile_reactor_network_steps_t2_kernel(
         for i in range(NV):
             c_tile = keep.tile([P, S], BF16, tag="c_in%d" % i, name="c_tile", align_bytes=64)
             c_sb.append(c_tile)
-        a_sb = keep.tile([P, NS, 2 * S], U8, align_bytes=64)
-        a_sc = keep.tile([P, NS, S], U8, align_bytes=64)
+        a_sb = []
+        for n in range(NS):
+            a_chunk = keep.tile([P, NS, 1024], U8, tag="a_chunk%d" % n, name="a_chunk", align_bytes=64)
+            a_sb.append(a_chunk)
+        a_sc_first = keep.tile([P, NS, 512], U8, align_bytes=64)
+        a_sc_rest = keep.tile([P, NS, S - 512], U8, align_bytes=64)
         f_raw = keep.tile([P, NG, 2 * V], U8, align_bytes=64)
         f_sb = keep.tile([P, NG, 2 * V], U8, align_bytes=64)
         fs_raw = keep.tile([P, NG, V], U8, align_bytes=64)
@@ -77,17 +82,17 @@ def tile_reactor_network_steps_t2_kernel(
             def load_c(i):
                 nc.sync.dma_start(out=c_sb[i][:], in_=c_rows[:, i // 4, i % 4, :])
 
-            def load_planes(plane, scales, lo, hi, queue=nc.sync):
+            def load_planes(plane, scales, lo, hi, queue):
                 for q in range(4):
                     queue.dma_start(
-                        out=plane[32 * q : 32 * q + 4, :, lo:hi].bitcast(I32),
+                        out=plane[32 * q : 32 * q + 4, :, :].bitcast(I32),
                         in_=scales[:, 4 * q : 4 * q + 4, lo:hi].rearrange("a r n -> r a n").bitcast(I32),
                     )
 
             def load_a(n):
                 cols = slice(1024 * n, 1024 * (n + 1))
                 nc.sync.dma_start(
-                    out=a_sb[:, :, cols].bitcast(I32),
+                    out=a_sb[n][:].bitcast(I32),
                     in_=a_words[:, :, cols].rearrange("a p w -> p a w").bitcast(I32),
                 )
 
@@ -96,21 +101,22 @@ def tile_reactor_network_steps_t2_kernel(
             nc.gpsimd.tensor_copy(out=ident_b[:], in_=ident[:])
             nc.scalar.dma_start(out=vt_rows[0:NG, :], in_=vol.rearrange("(g r) -> g r", g=NG))
             nc.scalar.dma_start(out=vt_rows[NG : 2 * NG, :], in_=theta.rearrange("(g r) -> g r", g=NG))
-            nc.vector.memset(a_sc[:].rearrange("p a n -> p (a n)").bitcast(I32), 0)
+            nc.vector.memset(a_sc_first[:].rearrange("p a n -> p (a n)").bitcast(I32), 0)
+            nc.vector.memset(a_sc_rest[:].rearrange("p a n -> p (a n)").bitcast(I32), 0)
             nc.gpsimd.memset(fs_raw[:].rearrange("p a n -> p (a n)").bitcast(I32), 0)
             nc.gpsimd.memset(b_sc[:].rearrange("p a n -> p (a n)").bitcast(I32), 0)
-            load_planes(a_sc, a_scales, 0, 512, nc.scalar)
             for i in range(4):
                 load_c(i)
+            load_planes(a_sc_first, a_scales, 0, 512, nc.sync)
             load_a(0)
             for i in range(4, NV):
                 load_c(i)
-            load_planes(fs_raw, f_scales, 0, V)
+            load_planes(fs_raw, f_scales, 0, V, nc.sync)
             nc.sync.dma_start(out=f_raw[:].bitcast(I32), in_=f_words.rearrange("g p w -> p g w").bitcast(I32))
-            load_planes(a_sc, a_scales, 512, S)
+            load_planes(a_sc_rest, a_scales, 512, S, nc.sync)
             load_a(1)
-            load_planes(b_sc, b_scales, 0, J)
             load_a(2)
+            load_planes(b_sc, b_scales, 0, J, nc.sync)
             nc.sync.dma_start(out=b_sb[:].bitcast(I32), in_=b_words.rearrange("g p w -> p g w").bitcast(I32))
             for g in range(NG):
                 nc.sync.dma_start(out=y_sb[:, 4 * g : 4 * g + 4, :], in_=y_rows[:, g, :, :])
@@ -141,19 +147,34 @@ def tile_reactor_network_steps_t2_kernel(
                     out=codes.bitcast(FP8X4), scales=scales, in_=grouped[:].rearrange("p r t -> p (r t)")
                 )
 
+            turned = {}
+
+            def shuffle_c(i):
+                words = keep.tile([P, 2, 384], I32, tag="c_words%d" % i, name="words", align_bytes=64)
+                turned[i] = words
+                if SHUF[i] == "vector":
+                    nc.vector.tensor_copy(
+                        out=words[:], in_=c_sb[i][:].bitcast(I32).rearrange("p (w u) -> p u w", u=2)
+                    )
+                else:
+                    nc.scalar.copy(
+                        out=words[:].bitcast(U32), in_=c_sb[i][:].bitcast(U32).rearrange("p (w u) -> p u w", u=2)
+                    )
+
             def transposes_c(j):
                 banks = []
-                c_words = [c_sb[2 * j + k][:].bitcast(F32) for k in range(2)]
                 for a in range(NS):
                     bank = psum.tile([P, 2, 2, P], F32, tag="bank", name="bank")
                     banks.append(bank)
                 for k in range(2):
+                    i = 2 * j + k
                     for a in range(NS):
                         for u in range(2):
-                            lo = 256 * a + u
-                            nc.tensor.transpose(
-                                banks[a][:, k, u, :], c_words[k][:, lo : 256 * (a + 1) : 2], ident[:]
-                            )
+                            if i in turned:
+                                part = turned[i][:, u, P * a : P * (a + 1)].bitcast(F32)
+                            else:
+                                part = c_sb[i][:].bitcast(F32)[:, 256 * a + u : 256 * (a + 1) : 2]
+                            nc.tensor.transpose(banks[a][:, k, u, :], part, ident[:])
                 later(0, evac_c, j, banks)
 
             def evac_c(j, banks):
@@ -177,8 +198,8 @@ def tile_reactor_network_steps_t2_kernel(
                         out=acc[:],
                         lhsT=cq[:, a, rows].bitcast(FP8X4),
                         lhsT_scale=cq_sc[:, a, rows],
-                        rhs=a_sb[:, a, 1024 * n : 1024 * (n + 1)].bitcast(FP4X4),
-                        rhs_scale=a_sc[:, a, 512 * n : 512 * (n + 1)],
+                        rhs=a_sb[n][:, a, :].bitcast(FP4X4),
+                        rhs_scale=a_sc_first[:, a, :] if n == 0 else a_sc_rest[:, a, 512 * (n - 1) : 512 * n],
                         start=(a == 0),
                         stop=(a == NS - 1),
                     )
@@ -327,86 +348,92 @@ def tile_reactor_network_steps_t2_kernel(
             unit(transposes_c, 1)
             vectors()
             unit(stage1, 0, 0)
+            shuffle_c(4)
             unit(stage1, 0, 1)
             unit(transposes_c, 2)
             unit(stage1, 0, 2)
             unit(stage1, 0, 3)
+            shuffle_c(7)
             unit(transposes_c, 3)
             unit(stage1, 0, 4)
-            permute_f(0, 0)
             unit(stage1, 0, 5)
-            permute_f(0, 1)
+            permute_f(0, 0)
             unit(stage1, 0, 6)
-            permute_f(0, 2)
+            permute_f(0, 1)
             unit(stage1, 0, 7)
-            permute_f(1, 0)
+            permute_f(0, 2)
             unit(stage1, 1, 0)
-            permute_f(1, 1)
+            permute_f(1, 0)
             unit(stage1, 1, 1)
-            permute_f(1, 2)
+            permute_f(1, 1)
             unit(stage1, 1, 2)
+            permute_f(1, 2)
             unit(stage1, 1, 3)
             unit(stage1, 1, 4)
             unit(stage1, 1, 5)
             unit(stage1, 1, 6)
             unit(stage1, 1, 7)
-            unit(stage2, 0, 0)
             unit(stage1, 2, 0)
-            unit(stage2, 0, 1)
+            unit(stage2, 0, 0)
             unit(stage1, 2, 1)
-            unit(stage2, 0, 2)
+            unit(stage2, 0, 1)
             unit(stage1, 2, 2)
-            unit(stage2, 0, 3)
+            unit(stage2, 0, 2)
             unit(stage1, 2, 3)
-            unit(stage2, 0, 4)
+            unit(stage2, 0, 3)
             unit(stage1, 2, 4)
-            unit(stage2, 0, 5)
+            unit(stage2, 0, 4)
             unit(stage1, 2, 5)
-            unit(stage2, 0, 6)
-            transposes_2(0, 0)
-            unit(transposes_2, 0, 1)
+            unit(stage2, 0, 5)
             unit(stage1, 2, 6)
-            unit(stage2, 0, 7)
+            unit(stage2, 0, 6)
             unit(stage1, 2, 7)
+            unit(stage2, 0, 7)
             unit(stage2, 1, 0)
             unit(stage2, 1, 1)
             unit(stage2, 1, 2)
             unit(stage2, 1, 3)
-            transposes_2(0, 2)
-            unit(transposes_2, 0, 3)
             unit(stage2, 1, 4)
             unit(stage2, 1, 5)
+            transposes_2(0, 0)
+            transposes_2(0, 1)
+            transposes_2(0, 2)
+            unit(transposes_2, 0, 3)
             unit(stage2, 1, 6)
-            transposes_2(1, 0)
-            unit(transposes_2, 1, 1)
             unit(stage2, 1, 7)
-            unit(transposes_2, 1, 2)
+            transposes_2(1, 0)
+            transposes_2(1, 1)
+            transposes_2(1, 2)
             unit(transposes_2, 1, 3)
             for k in range(2):
                             tick()
-            unit(stage3, 0, 0, 2)
-            unit(stage3, 1, 0, 2)
-            unit(stage3, 2, 0, 2)
-            unit(stage3, 3, 0, 2)
-            unit(stage2, 2, 0)
-            unit(stage2, 2, 1)
             unit(stage2, 2, 2)
+            unit(stage2, 2, 0)
+            unit(stage3, 1, 0, 2)
+            unit(stage3, 3, 0, 2)
+            unit(stage3, 0, 0, 2)
+            unit(stage2, 2, 1)
+            unit(stage3, 2, 0, 2)
             unit(stage2, 2, 3)
-            unit(stage2, 2, 4)
             unit(transposes_2, 2, 0)
+            unit(stage2, 2, 4)
             unit(stage2, 2, 5)
-            unit(stage2, 2, 6)
             unit(transposes_2, 2, 1)
-            unit(stage2, 2, 7)
+            unit(transposes_2, 2, 2)
+            unit(stage3, 7, 0, 2)
             unit(stage3, 0, 2, 3)
             unit(stage3, 1, 2, 3)
-            unit(transposes_2, 2, 2)
+            unit(stage2, 2, 6)
+            unit(stage2, 2, 7)
             unit(stage3, 2, 2, 3)
+            unit(stage3, 6, 0, 2)
             unit(stage3, 3, 2, 3)
             unit(transposes_2, 2, 3)
-            unit(stage3, 4, 0, 3)
-            unit(stage3, 5, 0, 3)
-            unit(stage3, 6, 0, 3)
-            unit(stage3, 7, 0, 3)
+            unit(stage3, 5, 0, 2)
+            unit(stage3, 4, 0, 2)
+            unit(stage3, 5, 2, 3)
+            unit(stage3, 7, 2, 3)
+            unit(stage3, 4, 2, 3)
+            unit(stage3, 6, 2, 3)
             for k in range(8):
                             tick()

@@ -20,13 +20,15 @@ EXP = mybir.ActivationFunctionType.Exp
 
 P = 128
 EVAC_C = ('vector', 'scalar', 'scalar')
-SHUF = (0, 0, 0, 0, 'scalar', 0, 0, 'vector')
-EVAC_2 = (('vector', 'scalar', 'scalar', 'scalar'), ('scalar', 'scalar', 'scalar', 'scalar'), ('vector', 'scalar', 'scalar', 'vector'))
-INTER = (('scalar', 'scalar', 'scalar', 'scalar'), ('scalar', 'scalar', 'scalar', 'vector'), ('scalar', 'scalar', 'scalar', 'scalar'))
+SHUF = (0, 0, 0, 'vector', 'scalar', 'scalar', 0, 'scalar')
+PERM = "gpsimd"
+FINISH = (0, 0, 0, 0, 0, 0, 0, 0)
+EVAC_2 = (('scalar', 'scalar', 'scalar', 'scalar'), ('scalar', 'scalar', 'scalar', 'scalar'), ('scalar', 'scalar', 'scalar', 'scalar'))
+INTER = (('scalar', 'vector', 'scalar', 'scalar'), ('scalar', 'scalar', 'scalar', 'vector'), ('scalar', 'scalar', 'scalar', 'scalar'))
 LAG_QC = 1
-LAG_M = 1
-LAG_I = (1, 1, 2, 2)
-LAG_QM = 6
+LAG_M = 2
+LAG_I = (1, 3, 4, 4)
+LAG_QM = 7
 LAG_Q2 = 3
 NV = V // P
 NS = S // 512
@@ -58,8 +60,8 @@ def tile_reactor_network_steps_t2_kernel(
         f_sc = keep.tile([P, NG, V], U8, align_bytes=64)
         b_sb = keep.tile([P, NS, 2 * J], U8, align_bytes=64)
         b_sc = keep.tile([P, NS, J], U8, align_bytes=64)
-        cq = keep.tile([P, NS, V], U32, align_bytes=64)
-        cq_sc = keep.tile([P, NS, V], U8, align_bytes=64)
+        cq = keep.tile([P, NV // 2, NS, 2 * P], U32, align_bytes=64)
+        cq_sc = keep.tile([P, NV // 2, NS, 2 * P], U8, align_bytes=64)
         mq = keep.tile([P, NS, NG, 512], U32, align_bytes=64)
         mq_sc = keep.tile([P, NS, NG, 512], U8, align_bytes=64)
         c2q = keep.tile([P, NS, V], U32, align_bytes=64)
@@ -107,16 +109,16 @@ def tile_reactor_network_steps_t2_kernel(
             nc.gpsimd.memset(b_sc[:].rearrange("p a n -> p (a n)").bitcast(I32), 0)
             for i in range(4):
                 load_c(i)
-            load_planes(a_sc_first, a_scales, 0, 512, nc.sync)
             load_a(0)
+            load_planes(a_sc_first, a_scales, 0, 512, nc.sync)
             for i in range(4, NV):
                 load_c(i)
             load_planes(fs_raw, f_scales, 0, V, nc.sync)
-            nc.sync.dma_start(out=f_raw[:].bitcast(I32), in_=f_words.rearrange("g p w -> p g w").bitcast(I32))
             load_planes(a_sc_rest, a_scales, 512, S, nc.sync)
+            load_planes(b_sc, b_scales, 0, J, nc.sync)
+            nc.sync.dma_start(out=f_raw[:].bitcast(I32), in_=f_words.rearrange("g p w -> p g w").bitcast(I32))
             load_a(1)
             load_a(2)
-            load_planes(b_sc, b_scales, 0, J, nc.sync)
             nc.sync.dma_start(out=b_sb[:].bitcast(I32), in_=b_words.rearrange("g p w -> p g w").bitcast(I32))
             for g in range(NG):
                 nc.sync.dma_start(out=y_sb[:, 4 * g : 4 * g + 4, :], in_=y_rows[:, g, :, :])
@@ -135,16 +137,22 @@ def tile_reactor_network_steps_t2_kernel(
                 clock[0] += 1
 
             def spread(bank, grouped, engine):
-                dst = grouped[:].bitcast(F32).rearrange("p (k r) u -> p k r u", k=2)
+                dst = grouped.bitcast(F32).rearrange("p (k r) u -> p k r u", k=2)
                 src = bank[:].rearrange("p k u r -> p k r u")
                 if engine == "scalar":
                     nc.scalar.copy(out=dst, in_=src)
                 else:
                     nc.vector.tensor_copy(out=dst, in_=src)
 
+            def new_group(count):
+                grouped = work.tile(
+                    [P, count, 2 * P, 4], BF16, tag="grouped%d" % count, name="grouped", bufs=4, align_bytes=64
+                )
+                return grouped
+
             def quant(grouped, codes, scales):
                 nc.vector.quantize_mx(
-                    out=codes.bitcast(FP8X4), scales=scales, in_=grouped[:].rearrange("p r t -> p (r t)")
+                    out=codes.bitcast(FP8X4), scales=scales, in_=grouped[:].rearrange("p k r t -> p (k r t)")
                 )
 
             turned = {}
@@ -178,26 +186,28 @@ def tile_reactor_network_steps_t2_kernel(
                 later(0, evac_c, j, banks)
 
             def evac_c(j, banks):
-                groups = []
+                first = new_group(2)
+                last = new_group(1)
                 for a in range(NS):
-                    grouped = work.tile([P, 2 * P, 4], BF16, tag="grouped", name="grouped", bufs=6, align_bytes=64)
-                    spread(banks[a], grouped, EVAC_C[a])
-                    groups.append(grouped)
-                later(LAG_QC, quant_c, j, groups)
+                    spread(banks[a], first[:, a, :, :] if a < 2 else last[:, 0, :, :], EVAC_C[a])
+                later(LAG_QC, quant_c, j, first, last)
 
-            def quant_c(j, groups):
-                cols = slice(2 * P * j, 2 * P * (j + 1))
-                for a in range(NS):
-                    quant(groups[a], cq[:, a, cols], cq_sc[:, a, cols])
+            def quant_c(j, first, last):
+                quant(
+                    first,
+                    cq[:, j, 0:2, :].rearrange("p a r -> p (a r)"),
+                    cq_sc[:, j, 0:2, :].rearrange("p a r -> p (a r)"),
+                )
+                quant(last, cq[:, j, 2, :], cq_sc[:, j, 2, :])
 
             def stage1(n, i):
                 acc = psum.tile([P, 512], F32, tag="bank", name="acc")
-                rows = slice(P * i, P * (i + 1))
+                rows = slice(P * (i % 2), P * (i % 2 + 1))
                 for a in range(NS):
                     nc.tensor.matmul_mx(
                         out=acc[:],
-                        lhsT=cq[:, a, rows].bitcast(FP8X4),
-                        lhsT_scale=cq_sc[:, a, rows],
+                        lhsT=cq[:, i // 2, a, rows].bitcast(FP8X4),
+                        lhsT_scale=cq_sc[:, i // 2, a, rows],
                         rhs=a_sb[n][:, a, :].bitcast(FP4X4),
                         rhs_scale=a_sc_first[:, a, :] if n == 0 else a_sc_rest[:, a, 512 * (n - 1) : 512 * n],
                         start=(a == 0),
@@ -227,15 +237,15 @@ def tile_reactor_network_steps_t2_kernel(
                     out=mlin[:, i % 4, :], in_=c1[:, i, cols], func=COPY, scale=vol_f[:, i : i + 1]
                 )
                 if i % 4 == 3:
-                    mint = work.tile([P, 512, 4], BF16, tag="mint", name="mint", bufs=2, align_bytes=64)
+                    mint = work.tile([P, 1, 512, 4], BF16, tag="mint", name="mint", bufs=2, align_bytes=64)
                     for h in range(4):
                         later(LAG_I[h], interleave, n, mlin, mint, h)
                     later(LAG_QM, quant_m, n, i // 4, mint)
 
             def interleave(n, mlin, mint, h):
                 cols = slice(128 * h, 128 * (h + 1))
-                dst = mint[:, cols, :]
-                src = mlin[:, :, cols].rearrange("p t s -> p s t")
+                dst = mint[:, 0, cols, :].rearrange("p (w i) t -> p w t i", i=4)
+                src = mlin[:, :, cols].rearrange("p t (w i) -> p w t i", i=4)
                 if INTER[n][h] == "scalar":
                     nc.scalar.copy(out=dst, in_=src)
                 else:
@@ -269,22 +279,27 @@ def tile_reactor_network_steps_t2_kernel(
                     out=c2[:, i % 2, :], in0=acc[:], in1=c1[:, i, 512 * n : 512 * (n + 1)], op=ADD
                 )
 
-            def transposes_2(n, j):
-                c2 = pairs[(n, j)]
-                words = c2[:].bitcast(F32)
-                bank = psum.tile([P, 2, 2, P], F32, tag="bank", name="bank")
-                for k in range(2):
-                    for u in range(2):
-                        nc.tensor.transpose(bank[:, k, u, :], words[:, k, P * u : P * (u + 1)], ident[:])
-                later(0, evac_2, n, j, bank)
+            def transposes_2(n, first, count):
+                banks = []
+                for j in range(first, first + count):
+                    words = pairs[(n, j)][:].bitcast(F32)
+                    bank = psum.tile([P, 2, 2, P], F32, tag="bank", name="bank")
+                    banks.append(bank)
+                    for k in range(2):
+                        for u in range(2):
+                            nc.tensor.transpose(bank[:, k, u, :], words[:, k, P * u : P * (u + 1)], ident[:])
+                later(0, evac_2, n, first, banks)
 
-            def evac_2(n, j, bank):
-                grouped = work.tile([P, 2 * P, 4], BF16, tag="grouped", name="grouped", bufs=6, align_bytes=64)
-                spread(bank, grouped, EVAC_2[n][j])
-                later(LAG_Q2, quant_2, n, j, grouped)
+            def evac_2(n, first, banks):
+                size = min(2, len(banks))
+                for lo in range(0, len(banks), size):
+                    grouped = new_group(size)
+                    for k in range(size):
+                        spread(banks[lo + k], grouped[:, k, :, :], EVAC_2[n][first + lo + k])
+                    later(LAG_Q2 + lo // 2, quant_2, n, first + lo, size, grouped)
 
-            def quant_2(n, j, grouped):
-                cols = slice(2 * P * j, 2 * P * (j + 1))
+            def quant_2(n, first, count, grouped):
+                cols = slice(2 * P * first, 2 * P * (first + count))
                 quant(grouped, c2q[:, n, cols], c2q_sc[:, n, cols])
 
             accs = {}
@@ -310,22 +325,28 @@ def tile_reactor_network_steps_t2_kernel(
 
             def finish(i, acc):
                 res = work.tile([P, 512], F32, tag="res", name="res", bufs=4, align_bytes=64)
-                nc.vector.scalar_tensor_tensor(
-                    out=res[:], in0=acc[:], scalar=gate[:, i : i + 1], in1=y_sb[:, i, :], op0=MULT, op1=ADD
-                )
+                if FINISH[i]:
+                    part = work.tile([P, 512], F32, tag="part", name="part", bufs=2, align_bytes=64)
+                    nc.scalar.activation(out=part[:], in_=acc[:], func=COPY, scale=gate[:, i : i + 1])
+                    nc.gpsimd.tensor_tensor(out=res[:], in0=part[:], in1=y_sb[:, i, :], op=ADD)
+                else:
+                    nc.vector.scalar_tensor_tensor(
+                        out=res[:], in0=acc[:], scalar=gate[:, i : i + 1], in1=y_sb[:, i, :], op0=MULT, op1=ADD
+                    )
                 nc.sync.dma_start(out=out_rows[:, i // 4, i % 4, :], in_=res[:])
 
             def permute_f(g, h):
+                move = nc.gpsimd if PERM == "gpsimd" else nc.vector
                 if h < 2:
                     cols = slice(1024 * h, 1024 * (h + 1))
-                    nc.vector.tensor_copy(
+                    move.tensor_copy(
                         out=f_sb[:, g, cols].rearrange("p (t m b) -> p t m b", t=4, b=2),
                         in_=f_raw[:, g, cols].rearrange("p (m t b) -> p t m b", t=4, b=2),
                     )
                 else:
                     for h2 in range(2):
                         cols = slice(512 * h2, 512 * (h2 + 1))
-                        nc.vector.tensor_copy(
+                        move.tensor_copy(
                             out=f_sc[:, g, cols].rearrange("p (t m) -> p t m", t=4),
                             in_=fs_raw[:, g, cols].rearrange("p (m t) -> p t m", t=4),
                         )
@@ -345,11 +366,13 @@ def tile_reactor_network_steps_t2_kernel(
                 tick()
 
             unit(transposes_c, 0)
+            shuffle_c(3)
             unit(transposes_c, 1)
             vectors()
             unit(stage1, 0, 0)
             shuffle_c(4)
             unit(stage1, 0, 1)
+            shuffle_c(5)
             unit(transposes_c, 2)
             unit(stage1, 0, 2)
             unit(stage1, 0, 3)
@@ -357,20 +380,20 @@ def tile_reactor_network_steps_t2_kernel(
             unit(transposes_c, 3)
             unit(stage1, 0, 4)
             unit(stage1, 0, 5)
-            permute_f(0, 0)
             unit(stage1, 0, 6)
-            permute_f(0, 1)
             unit(stage1, 0, 7)
-            permute_f(0, 2)
             unit(stage1, 1, 0)
-            permute_f(1, 0)
+            permute_f(0, 0)
             unit(stage1, 1, 1)
-            permute_f(1, 1)
+            permute_f(0, 1)
             unit(stage1, 1, 2)
-            permute_f(1, 2)
+            permute_f(0, 2)
             unit(stage1, 1, 3)
+            permute_f(1, 0)
             unit(stage1, 1, 4)
+            permute_f(1, 1)
             unit(stage1, 1, 5)
+            permute_f(1, 2)
             unit(stage1, 1, 6)
             unit(stage1, 1, 7)
             unit(stage1, 2, 0)
@@ -395,45 +418,39 @@ def tile_reactor_network_steps_t2_kernel(
             unit(stage2, 1, 3)
             unit(stage2, 1, 4)
             unit(stage2, 1, 5)
-            transposes_2(0, 0)
-            transposes_2(0, 1)
-            transposes_2(0, 2)
-            unit(transposes_2, 0, 3)
+            unit(transposes_2, 0, 0, 4)
             unit(stage2, 1, 6)
             unit(stage2, 1, 7)
-            transposes_2(1, 0)
-            transposes_2(1, 1)
-            transposes_2(1, 2)
-            unit(transposes_2, 1, 3)
+            unit(transposes_2, 1, 0, 4)
             for k in range(2):
                             tick()
-            unit(stage2, 2, 2)
             unit(stage2, 2, 0)
+            unit(stage2, 2, 2)
+            unit(stage2, 2, 3)
+            unit(stage2, 2, 1)
+            unit(stage2, 2, 4)
+            unit(stage3, 0, 0, 2)
+            unit(stage2, 2, 6)
+            unit(stage3, 2, 0, 2)
+            unit(transposes_2, 2, 0, 1)
+            unit(transposes_2, 2, 1, 1)
             unit(stage3, 1, 0, 2)
             unit(stage3, 3, 0, 2)
-            unit(stage3, 0, 0, 2)
-            unit(stage2, 2, 1)
-            unit(stage3, 2, 0, 2)
-            unit(stage2, 2, 3)
-            unit(transposes_2, 2, 0)
-            unit(stage2, 2, 4)
-            unit(stage2, 2, 5)
-            unit(transposes_2, 2, 1)
-            unit(transposes_2, 2, 2)
-            unit(stage3, 7, 0, 2)
             unit(stage3, 0, 2, 3)
-            unit(stage3, 1, 2, 3)
-            unit(stage2, 2, 6)
-            unit(stage2, 2, 7)
             unit(stage3, 2, 2, 3)
-            unit(stage3, 6, 0, 2)
+            unit(stage2, 2, 5)
+            unit(stage2, 2, 7)
             unit(stage3, 3, 2, 3)
-            unit(transposes_2, 2, 3)
+            unit(stage3, 1, 2, 3)
+            unit(transposes_2, 2, 2, 1)
+            unit(transposes_2, 2, 3, 1)
             unit(stage3, 5, 0, 2)
             unit(stage3, 4, 0, 2)
-            unit(stage3, 5, 2, 3)
-            unit(stage3, 7, 2, 3)
             unit(stage3, 4, 2, 3)
+            unit(stage3, 6, 0, 2)
             unit(stage3, 6, 2, 3)
+            unit(stage3, 5, 2, 3)
+            unit(stage3, 7, 0, 2)
+            unit(stage3, 7, 2, 3)
             for k in range(8):
                             tick()

from contextlib import ExitStack

import concourse.mybir as mybir
from concourse.masks import make_identity

V, S, J = 1024, 1536, 512
FLOPS = 2 * V * S * S + 2 * V * V * S + 2 * V * S * J

F32 = mybir.dt.float32
BF16 = mybir.dt.bfloat16
I32 = mybir.dt.int32
U32 = mybir.dt.uint32
U8 = mybir.dt.uint8
FP8X4 = mybir.dt.float8_e4m3fn_x4
FP4X4 = mybir.dt.float4_e2m1fn_x4
ADD = mybir.AluOpType.add
MULT = mybir.AluOpType.mult
COPY = mybir.ActivationFunctionType.Copy
EXP = mybir.ActivationFunctionType.Exp

P = 128
EVAC_C = ('vector', 'scalar', 'scalar')
SHUF = (0, 0, 0, 'vector', 'scalar', 'scalar', 0, 'scalar')
PERM = "gpsimd"
FINISH = (0, 0, 0, 0, 0, 0, 0, 0)
EVAC_2 = (('scalar', 'scalar', 'scalar', 'scalar'), ('scalar', 'scalar', 'scalar', 'scalar'), ('scalar', 'scalar', 'scalar', 'scalar'))
INTER = (('scalar', 'vector', 'scalar', 'scalar'), ('scalar', 'scalar', 'scalar', 'vector'), ('scalar', 'scalar', 'scalar', 'scalar'))
LAG_QC = 1
LAG_M = 2
LAG_I = (1, 3, 4, 4)
LAG_QM = 7
LAG_Q2 = 3
NV = V // P
NS = S // 512
NG = V // 512


def tile_reactor_network_steps_t2_kernel(
    tc, c, a_words, a_scales, vol, f_words, f_scales, b_words, b_scales, theta, y0, out
):
    nc = tc.nc
    with ExitStack() as ctx:
        keep = ctx.enter_context(tc.tile_pool(name="keep", bufs=1))
        work = ctx.enter_context(tc.tile_pool(name="work", bufs=2))
        psum = ctx.enter_context(tc.psum_pool(name="psum", bufs=8))

        c_sb = []
        for i in range(NV):
            c_tile = keep.tile([P, S], BF16, tag="c_in%d" % i, name="c_tile", align_bytes=64)
            c_sb.append(c_tile)
        a_sb = []
        for n in range(NS):
            a_chunk = keep.tile([P, NS, 1024], U8, tag="a_chunk%d" % n, name="a_chunk", align_bytes=64)
            a_sb.append(a_chunk)
        a_sc_first = keep.tile([P, NS, 512], U8, align_bytes=64)
        a_sc_rest = keep.tile([P, NS, S - 512], U8, align_bytes=64)
        f_raw = keep.tile([P, NG, 2 * V], U8, align_bytes=64)
        f_sb = keep.tile([P, NG, 2 * V], U8, align_bytes=64)
        fs_raw = keep.tile([P, NG, V], U8, align_bytes=64)
        f_sc = keep.tile([P, NG, V], U8, align_bytes=64)
        b_sb = keep.tile([P, NS, 2 * J], U8, align_bytes=64)
        b_sc = keep.tile([P, NS, J], U8, align_bytes=64)
        cq = keep.tile([P, NV // 2, NS, 2 * P], U32, align_bytes=64)
        cq_sc = keep.tile([P, NV // 2, NS, 2 * P], U8, align_bytes=64)
        mq = keep.tile([P, NS, NG, 512], U32, align_bytes=64)
        mq_sc = keep.tile([P, NS, NG, 512], U8, align_bytes=64)
        c2q = keep.tile([P, NS, V], U32, align_bytes=64)
        c2q_sc = keep.tile([P, NS, V], U8, align_bytes=64)
        c1 = keep.tile([P, NV, S], F32, align_bytes=64)
        y_sb = keep.tile([P, NV, J], BF16, align_bytes=64)
        ident = keep.tile([P, P], F32, align_bytes=64)
        ident_b = keep.tile([P, P], BF16, align_bytes=64)
        vt_rows = keep.tile([P, 512], BF16, align_bytes=64)
        vt_cols = keep.tile([P, 2, NV], F32)
        vol_f = vt_cols[:, 0, :]
        gate = keep.tile([P, NV], F32)
        warm = keep.tile([P, 1], F32)

        with tc.manual_schedule():
            c_rows = c.rearrange("(g p t) s -> p g t s", p=P, t=4)
            y_rows = y0.rearrange("(g p t) j -> p g t j", p=P, t=4)
            out_rows = out.rearrange("(g p t) j -> p g t j", p=P, t=4)

            def load_c(i):
                nc.sync.dma_start(out=c_sb[i][:], in_=c_rows[:, i // 4, i % 4, :])

            def load_planes(plane, scales, lo, hi, queue):
                for q in range(4):
                    queue.dma_start(
                        out=plane[32 * q : 32 * q + 4, :, :].bitcast(I32),
                        in_=scales[:, 4 * q : 4 * q + 4, lo:hi].rearrange("a r n -> r a n").bitcast(I32),
                    )

            def load_a(n):
                cols = slice(1024 * n, 1024 * (n + 1))
                nc.sync.dma_start(
                    out=a_sb[n][:].bitcast(I32),
                    in_=a_words[:, :, cols].rearrange("a p w -> p a w").bitcast(I32),
                )

            nc.vector.memset(vt_rows[:], 0.0)
            make_identity(nc, ident[:])
            nc.gpsimd.tensor_copy(out=ident_b[:], in_=ident[:])
            nc.scalar.dma_start(out=vt_rows[0:NG, :], in_=vol.rearrange("(g r) -> g r", g=NG))
            nc.scalar.dma_start(out=vt_rows[NG : 2 * NG, :], in_=theta.rearrange("(g r) -> g r", g=NG))
            nc.vector.memset(a_sc_first[:].rearrange("p a n -> p (a n)").bitcast(I32), 0)
            nc.vector.memset(a_sc_rest[:].rearrange("p a n -> p (a n)").bitcast(I32), 0)
            nc.gpsimd.memset(fs_raw[:].rearrange("p a n -> p (a n)").bitcast(I32), 0)
            nc.gpsimd.memset(b_sc[:].rearrange("p a n -> p (a n)").bitcast(I32), 0)
            for i in range(4):
                load_c(i)
            load_a(0)
            load_planes(a_sc_first, a_scales, 0, 512, nc.sync)
            for i in range(4, NV):
                load_c(i)
            load_planes(fs_raw, f_scales, 0, V, nc.sync)
            load_planes(a_sc_rest, a_scales, 512, S, nc.sync)
            load_planes(b_sc, b_scales, 0, J, nc.sync)
            nc.sync.dma_start(out=f_raw[:].bitcast(I32), in_=f_words.rearrange("g p w -> p g w").bitcast(I32))
            load_a(1)
            load_a(2)
            nc.sync.dma_start(out=b_sb[:].bitcast(I32), in_=b_words.rearrange("g p w -> p g w").bitcast(I32))
            for g in range(NG):
                nc.sync.dma_start(out=y_sb[:, 4 * g : 4 * g + 4, :], in_=y_rows[:, g, :, :])
            nc.vector.memset(warm[:], 0.0)
            nc.scalar.activation(out=warm[:], in_=warm[:], func=EXP)

            todo = {}
            clock = [0]

            def later(lag, fn, *args):
                todo.setdefault(clock[0] + lag, []).append((fn, args))

            def tick():
                for fn, args in todo.get(clock[0], []):
                    fn(*args)
                clock[0] += 1

            def spread(bank, grouped, engine):
                dst = grouped.bitcast(F32).rearrange("p (k r) u -> p k r u", k=2)
                src = bank[:].rearrange("p k u r -> p k r u")
                if engine == "scalar":
                    nc.scalar.copy(out=dst, in_=src)
                else:
                    nc.vector.tensor_copy(out=dst, in_=src)

            def new_group(count):
                grouped = work.tile(
                    [P, count, 2 * P, 4], BF16, tag="grouped%d" % count, name="grouped", bufs=4, align_bytes=64
                )
                return grouped

            def quant(grouped, codes, scales):
                nc.vector.quantize_mx(
                    out=codes.bitcast(FP8X4), scales=scales, in_=grouped[:].rearrange("p k r t -> p (k r t)")
                )

            turned = {}

            def shuffle_c(i):
                words = keep.tile([P, 2, 384], I32, tag="c_words%d" % i, name="words", align_bytes=64)
                turned[i] = words
                if SHUF[i] == "vector":
                    nc.vector.tensor_copy(
                        out=words[:], in_=c_sb[i][:].bitcast(I32).rearrange("p (w u) -> p u w", u=2)
                    )
                else:
                    nc.scalar.copy(
                        out=words[:].bitcast(U32), in_=c_sb[i][:].bitcast(U32).rearrange("p (w u) -> p u w", u=2)
                    )

            def transposes_c(j):
                banks = []
                for a in range(NS):
                    bank = psum.tile([P, 2, 2, P], F32, tag="bank", name="bank")
                    banks.append(bank)
                for k in range(2):
                    i = 2 * j + k
                    for a in range(NS):
                        for u in range(2):
                            if i in turned:
                                part = turned[i][:, u, P * a : P * (a + 1)].bitcast(F32)
                            else:
                                part = c_sb[i][:].bitcast(F32)[:, 256 * a + u : 256 * (a + 1) : 2]
                            nc.tensor.transpose(banks[a][:, k, u, :], part, ident[:])
                later(0, evac_c, j, banks)

            def evac_c(j, banks):
                first = new_group(2)
                last = new_group(1)
                for a in range(NS):
                    spread(banks[a], first[:, a, :, :] if a < 2 else last[:, 0, :, :], EVAC_C[a])
                later(LAG_QC, quant_c, j, first, last)

            def quant_c(j, first, last):
                quant(
                    first,
                    cq[:, j, 0:2, :].rearrange("p a r -> p (a r)"),
                    cq_sc[:, j, 0:2, :].rearrange("p a r -> p (a r)"),
                )
                quant(last, cq[:, j, 2, :], cq_sc[:, j, 2, :])

            def stage1(n, i):
                acc = psum.tile([P, 512], F32, tag="bank", name="acc")
                rows = slice(P * (i % 2), P * (i % 2 + 1))
                for a in range(NS):
                    nc.tensor.matmul_mx(
                        out=acc[:],
                        lhsT=cq[:, i // 2, a, rows].bitcast(FP8X4),
                        lhsT_scale=cq_sc[:, i // 2, a, rows],
                        rhs=a_sb[n][:, a, :].bitcast(FP4X4),
                        rhs_scale=a_sc_first[:, a, :] if n == 0 else a_sc_rest[:, a, 512 * (n - 1) : 512 * n],
                        start=(a == 0),
                        stop=(a == NS - 1),
                    )
                later(0, add_c, n, i, acc)

            mlins = {}

            def add_c(n, i, acc):
                cols = slice(512 * n, 512 * (n + 1))
                nc.vector.tensor_tensor(
                    out=c1[:, i, cols].rearrange("p (u w e) -> p u w e", u=2, e=2),
                    in0=acc[:].rearrange("p (w u e) -> p u w e", u=2, e=2),
                    in1=c_sb[i][:, cols].rearrange("p (w u e) -> p u w e", u=2, e=2),
                    op=ADD,
                )
                later(LAG_M, amounts, n, i)

            def amounts(n, i):
                cols = slice(512 * n, 512 * (n + 1))
                if i % 4 == 0:
                    mlin = work.tile([P, 4, 512], BF16, tag="mlin", name="mlin", bufs=2, align_bytes=64)
                    mlins[0] = mlin
                mlin = mlins[0]
                nc.scalar.activation(
                    out=mlin[:, i % 4, :], in_=c1[:, i, cols], func=COPY, scale=vol_f[:, i : i + 1]
                )
                if i % 4 == 3:
                    mint = work.tile([P, 1, 512, 4], BF16, tag="mint", name="mint", bufs=2, align_bytes=64)
                    for h in range(4):
                        later(LAG_I[h], interleave, n, mlin, mint, h)
                    later(LAG_QM, quant_m, n, i // 4, mint)

            def interleave(n, mlin, mint, h):
                cols = slice(128 * h, 128 * (h + 1))
                dst = mint[:, 0, cols, :].rearrange("p (w i) t -> p w t i", i=4)
                src = mlin[:, :, cols].rearrange("p t (w i) -> p w t i", i=4)
                if INTER[n][h] == "scalar":
                    nc.scalar.copy(out=dst, in_=src)
                else:
                    nc.vector.tensor_copy(out=dst, in_=src)

            def quant_m(n, g, mint):
                quant(mint, mq[:, n, g, :], mq_sc[:, n, g, :])

            pairs = {}

            def stage2(n, i):
                acc = psum.tile([P, 512], F32, tag="bank", name="acc")
                for g in range(NG):
                    nc.tensor.matmul_mx(
                        out=acc[:],
                        lhsT=f_sb[:, g, 256 * i : 256 * (i + 1)].bitcast(FP4X4),
                        lhsT_scale=f_sc[:, g, P * i : P * (i + 1)],
                        rhs=mq[:, n, g, :].bitcast(FP8X4),
                        rhs_scale=mq_sc[:, n, g, :],
                        start=(g == 0),
                        stop=(g == NG - 1),
                    )
                later(0, add_c1, n, i, acc)

            def add_c1(n, i, acc):
                if i % 2 == 0:
                    c2 = work.tile([P, 2, 512], BF16, tag="c2", name="c2", bufs=8, align_bytes=64)
                    pairs[(n, i // 2)] = c2
                c2 = pairs[(n, i // 2)]
                nc.vector.tensor_tensor(
                    out=c2[:, i % 2, :], in0=acc[:], in1=c1[:, i, 512 * n : 512 * (n + 1)], op=ADD
                )

            def transposes_2(n, first, count):
                banks = []
                for j in range(first, first + count):
                    words = pairs[(n, j)][:].bitcast(F32)
                    bank = psum.tile([P, 2, 2, P], F32, tag="bank", name="bank")
                    banks.append(bank)
                    for k in range(2):
                        for u in range(2):
                            nc.tensor.transpose(bank[:, k, u, :], words[:, k, P * u : P * (u + 1)], ident[:])
                later(0, evac_2, n, first, banks)

            def evac_2(n, first, banks):
                size = min(2, len(banks))
                for lo in range(0, len(banks), size):
                    grouped = new_group(size)
                    for k in range(size):
                        spread(banks[lo + k], grouped[:, k, :, :], EVAC_2[n][first + lo + k])
                    later(LAG_Q2 + lo // 2, quant_2, n, first + lo, size, grouped)

            def quant_2(n, first, count, grouped):
                cols = slice(2 * P * first, 2 * P * (first + count))
                quant(grouped, c2q[:, n, cols], c2q_sc[:, n, cols])

            accs = {}

            def stage3(i, first, last):
                if first == 0:
                    acc = psum.tile([P, 512], F32, tag="bank", name="acc")
                    accs[i] = acc
                acc = accs[i]
                rows = slice(P * i, P * (i + 1))
                for n in range(first, last):
                    nc.tensor.matmul_mx(
                        out=acc[:],
                        lhsT=c2q[:, n, rows].bitcast(FP8X4),
                        lhsT_scale=c2q_sc[:, n, rows],
                        rhs=b_sb[:, n, :].bitcast(FP4X4),
                        rhs_scale=b_sc[:, n, :],
                        start=(n == 0),
                        stop=(n == NS - 1),
                    )
                if last == NS:
                    later(0, finish, i, acc)

            def finish(i, acc):
                res = work.tile([P, 512], F32, tag="res", name="res", bufs=4, align_bytes=64)
                if FINISH[i]:
                    part = work.tile([P, 512], F32, tag="part", name="part", bufs=2, align_bytes=64)
                    nc.scalar.activation(out=part[:], in_=acc[:], func=COPY, scale=gate[:, i : i + 1])
                    nc.gpsimd.tensor_tensor(out=res[:], in0=part[:], in1=y_sb[:, i, :], op=ADD)
                else:
                    nc.vector.scalar_tensor_tensor(
                        out=res[:], in0=acc[:], scalar=gate[:, i : i + 1], in1=y_sb[:, i, :], op0=MULT, op1=ADD
                    )
                nc.sync.dma_start(out=out_rows[:, i // 4, i % 4, :], in_=res[:])

            def permute_f(g, h):
                move = nc.gpsimd if PERM == "gpsimd" else nc.vector
                if h < 2:
                    cols = slice(1024 * h, 1024 * (h + 1))
                    move.tensor_copy(
                        out=f_sb[:, g, cols].rearrange("p (t m b) -> p t m b", t=4, b=2),
                        in_=f_raw[:, g, cols].rearrange("p (m t b) -> p t m b", t=4, b=2),
                    )
                else:
                    for h2 in range(2):
                        cols = slice(512 * h2, 512 * (h2 + 1))
                        move.tensor_copy(
                            out=f_sc[:, g, cols].rearrange("p (t m) -> p t m", t=4),
                            in_=fs_raw[:, g, cols].rearrange("p (m t) -> p t m", t=4),
                        )

            def vectors():
                bank = psum.tile([P, 4, P], BF16, tag="bank", name="bank")
                for k in range(4):
                    nc.tensor.transpose(bank[:, k, :], vt_rows[:, k:512:4], ident_b[:])
                nc.vector.tensor_copy(
                    out=vt_cols[:].rearrange("p v (g t) -> p v g t", g=NG),
                    in_=bank[:, :, 0 : 2 * NG].rearrange("p t (v g) -> p v g t", g=NG),
                )
                nc.scalar.activation(out=gate[:], in_=vt_cols[:, 1, :], func=EXP)

            def unit(fn, *args):
                fn(*args)
                tick()

            unit(transposes_c, 0)
            shuffle_c(3)
            unit(transposes_c, 1)
            vectors()
            unit(stage1, 0, 0)
            shuffle_c(4)
            unit(stage1, 0, 1)
            shuffle_c(5)
            unit(transposes_c, 2)
            unit(stage1, 0, 2)
            unit(stage1, 0, 3)
            shuffle_c(7)
            unit(transposes_c, 3)
            unit(stage1, 0, 4)
            unit(stage1, 0, 5)
            unit(stage1, 0, 6)
            unit(stage1, 0, 7)
            unit(stage1, 1, 0)
            permute_f(0, 0)
            unit(stage1, 1, 1)
            permute_f(0, 1)
            unit(stage1, 1, 2)
            permute_f(0, 2)
            unit(stage1, 1, 3)
            permute_f(1, 0)
            unit(stage1, 1, 4)
            permute_f(1, 1)
            unit(stage1, 1, 5)
            permute_f(1, 2)
            unit(stage1, 1, 6)
            unit(stage1, 1, 7)
            unit(stage1, 2, 0)
            unit(stage2, 0, 0)
            unit(stage1, 2, 1)
            unit(stage2, 0, 1)
            unit(stage1, 2, 2)
            unit(stage2, 0, 2)
            unit(stage1, 2, 3)
            unit(stage2, 0, 3)
            unit(stage1, 2, 4)
            unit(stage2, 0, 4)
            unit(stage1, 2, 5)
            unit(stage2, 0, 5)
            unit(stage1, 2, 6)
            unit(stage2, 0, 6)
            unit(stage1, 2, 7)
            unit(stage2, 0, 7)
            unit(stage2, 1, 0)
            unit(stage2, 1, 1)
            unit(stage2, 1, 2)
            unit(stage2, 1, 3)
            unit(stage2, 1, 4)
            unit(stage2, 1, 5)
            unit(transposes_2, 0, 0, 4)
            unit(stage2, 1, 6)
            unit(stage2, 1, 7)
            unit(transposes_2, 1, 0, 4)
            for k in range(2):
                            tick()
            unit(stage2, 2, 0)
            unit(stage2, 2, 2)
            unit(stage2, 2, 3)
            unit(stage2, 2, 1)
            unit(stage2, 2, 4)
            unit(stage3, 0, 0, 2)
            unit(stage2, 2, 6)
            unit(stage3, 2, 0, 2)
            unit(transposes_2, 2, 0, 1)
            unit(transposes_2, 2, 1, 1)
            unit(stage3, 1, 0, 2)
            unit(stage3, 3, 0, 2)
            unit(stage3, 0, 2, 3)
            unit(stage3, 2, 2, 3)
            unit(stage2, 2, 5)
            unit(stage2, 2, 7)
            unit(stage3, 3, 2, 3)
            unit(stage3, 1, 2, 3)
            unit(transposes_2, 2, 2, 1)
            unit(transposes_2, 2, 3, 1)
            unit(stage3, 5, 0, 2)
            unit(stage3, 4, 0, 2)
            unit(stage3, 4, 2, 3)
            unit(stage3, 6, 0, 2)
            unit(stage3, 6, 2, 3)
            unit(stage3, 5, 2, 3)
            unit(stage3, 7, 0, 2)
            unit(stage3, 7, 2, 3)
            for k in range(8):
                            tick()
